import numpy as np
import ml_dtypes


def mxq(x, axis, fmt="e4m3"):
    dtype, down = {"e4m3": (ml_dtypes.float8_e4m3fn, 7), "e5m2": (ml_dtypes.float8_e5m2, 14)}[fmt]
    v = np.moveaxis(np.asarray(x, np.float32).astype(ml_dtypes.bfloat16).astype(np.float64), axis, -1)
    blocks = v.reshape(v.shape[:-1] + (-1, 32))
    amax = np.abs(blocks).max(-1, keepdims=True)
    byte = np.maximum(np.where(amax > 0, np.frexp(amax)[1] - 1 + 127, 0) - down, 1)
    scale = np.exp2(byte - 127.0)
    codes = (blocks / scale).astype(np.float32).astype(dtype).astype(np.float64)
    return np.moveaxis((codes * scale).reshape(v.shape), -1, axis)


WIDE = False


def mx_kscale(k):
    if not WIDE:
        return np.ones(k)
    levels = np.array([30, -30])
    if k % 512:
        return np.exp2(np.random.permutation(np.resize(levels, k // 32))).repeat(32)
    a = np.empty((k // 512, 16))
    for p in range(k // 512):
        a[p, :8] = np.random.permutation(np.resize(levels, 8))
        for g in range(8):
            far = levels[np.abs(levels - a[p, g]) >= 10]
            a[p, g + 8] = far[np.random.randint(len(far))]
    return np.exp2(a.ravel()).repeat(32)


def f64(x):
    return np.asarray(x).astype(np.float64)


def striped(idx):
    return np.tile(np.asarray(idx).reshape(-1, 16).T, (8, 1)).astype(np.uint16)


def unstriped(offs):
    return offs[:16].T.reshape(-1).astype(np.int64)


E2M1 = np.array([0.0, 0.5, 1.0, 1.5, 2.0, 3.0, 4.0, 6.0, -0.0, -0.5, -1.0, -1.5, -2.0, -3.0, -4.0, -6.0])


def pack_weight(w, fmt):
    k, n = w.shape
    w = f64(np.asarray(w, np.float32).astype(ml_dtypes.bfloat16)).reshape(k // 32, 32, n)
    amax = np.abs(w).max(1)
    if fmt in ("e4m3", "e5m2"):
        byte = np.frexp(amax)[1] - 1 + 127 - (7 if fmt == "e4m3" else 14)
    else:
        mant, ex = np.frexp(amax / 6.0)
        byte = np.where(mant > 0.5, ex, ex - 1) + 127
    byte = np.clip(np.where(amax > 0, byte, 1), 1, 254)
    scaled = (w * np.exp2(127.0 - byte)[:, None, :]).reshape(k, n).astype(np.float32)
    by_word = np.ascontiguousarray(scaled.reshape(k // 512, 128, 4, n).transpose(0, 1, 3, 2))
    if fmt in ("e4m3", "e5m2"):
        words = by_word.astype(ml_dtypes.float8_e4m3fn if fmt == "e4m3" else ml_dtypes.float8_e5m2).view(np.uint8)
    else:
        c = by_word.astype(ml_dtypes.float4_e2m1fn).view(np.uint8) & 0xF
        words = (c[..., 0::2] | (c[..., 1::2] << 4)).reshape(k // 512, 128, 2 * n)
    return np.ascontiguousarray(words), np.ascontiguousarray(byte.astype(np.uint8).reshape(k // 512, 16, n))


def unpack_weight(words, scales, fmt):
    g, _, n = scales.shape
    words = np.ascontiguousarray(words).reshape(g, 128, n, -1)
    if fmt in ("e4m3", "e5m2"):
        vals = words.view(ml_dtypes.float8_e4m3fn if fmt == "e4m3" else ml_dtypes.float8_e5m2).astype(np.float64)
    else:
        nib = np.empty((g, 128, n, 4), np.uint8)
        nib[..., 0::2] = words & 0xF
        nib[..., 1::2] = words >> 4
        vals = E2M1[nib]
    vals = vals * np.repeat(np.exp2(scales.astype(np.float64) - 127.0), 8, axis=1)[..., None]
    return vals.transpose(0, 1, 3, 2).reshape(g * 512, n)


K, T, J, R, N, C = 1024, 1024, 384, 512, 256, 1024


def setup_inputs():
    n = np.random.standard_normal
    idx = np.random.permutation(T)[:J]
    idx2 = np.random.permutation(T)[:J]
    idx3 = np.random.permutation(C)[:J]
    fk = mx_kscale(K)
    fr = mx_kscale(R)
    wp = pack_weight(n((K, R)) * 1 / np.sqrt(K) * fk[:, None] * fr, "e2m1")
    wbp = pack_weight(n((R, N)) * 1 / np.sqrt(R) / fr[:, None], "e5m2")
    return {
        "xf": (n((K, T))).astype(np.float32),
        "fk": (np.random.uniform(0.5, 2.0, (K, 1)) / fk[:, None]).astype(np.float32),
        "w_words": wp[0],
        "w_scales": wp[1],
        "us": (np.random.uniform(0.5, 2.0, (R, 1)) * fr[:, None]).astype(np.float32),
        "wb_words": wbp[0],
        "wb_scales": wbp[1],
        "old": (1.0 * n((N, C))).astype(np.float32),
        "offs": striped(idx),
        "offs2": striped(idx2),
        "offs3": striped(idx3),
    }


def reference(xf, fk, w_words, w_scales, us, wb_words, wb_scales, old, offs, offs2, offs3):
    idx = unstriped(offs)
    idx2 = unstriped(offs2)
    idx3 = unstriped(offs3)
    wu = unpack_weight(w_words, w_scales, "e2m1")
    wbu = unpack_weight(wb_words, wb_scales, "e5m2")
    u = (f64(xf)[:, idx] - f64(xf)[:, idx2]) * f64(fk)
    uq = mxq(u, 0, "e4m3")
    a = wu.T @ uq
    pk1 = np.max(np.abs(a), axis=1, keepdims=True)
    hid = a / pk1 * f64(us)
    hidq = mxq(hid, 0, "e4m3")
    p = wbu.T @ hidq
    pp = np.zeros((N, C))
    pp[:, idx3] = p
    y = pp + 0.5 * f64(old)
    return y

@@ -1,0 +1,245 @@
+from contextlib import ExitStack
+
+import concourse.mybir as mybir
+
+K, T, J, R, N, C = 1024, 1024, 384, 512, 256, 1024
+FLOPS = 2 * K * R * J + 2 * R * N * J
+
+F32 = mybir.dt.float32
+BF16 = mybir.dt.bfloat16
+I32 = mybir.dt.int32
+U32 = mybir.dt.uint32
+U16 = mybir.dt.uint16
+U8 = mybir.dt.uint8
+E4M3 = mybir.dt.float8_e4m3fn_x4
+E5M2 = mybir.dt.float8_e5m2_x4
+E2M1 = mybir.dt.float4_e2m1fn_x4
+ALU = mybir.AluOpType
+ACT = mybir.ActivationFunctionType
+AXIS = mybir.AxisListType
+
+P = 128
+PACK = 4
+PASSES = K // (P * PACK)
+CH = 128
+CHUNKS = J // CH
+NT = N // P
+LIST_COLS = J // 16
+CH_COLS = CH // 16
+BOTH_ON_SCALAR = (4,)
+
+
+def tile_list_pickgaps_peakscaled_scattered_kernel(
+    tc, xf, fk, w_words, w_scales, us, wb_words, wb_scales, old, offs, offs2, offs3, out
+):
+    nc = tc.nc
+    with ExitStack() as ctx:
+        keep = ctx.enter_context(tc.tile_pool(name="keep", bufs=1))
+        psum = ctx.enter_context(tc.psum_pool(name="psum", bufs=1))
+
+        def sb(name, shape, dtype):
+            return keep.tile(shape, dtype, name=name, align_bytes=64)
+
+        first = keep.tile([P, LIST_COLS], U16, name="first")
+        second = keep.tile([P, LIST_COLS], U16, name="second")
+        places = keep.tile([P, LIST_COLS], U16, name="places")
+        planes = [[sb(f"x{a}{t}", [P, T], F32) for t in range(PACK)] for a in range(PASSES)]
+        x_rows = xf.rearrange("(a p t) c -> a t p c", a=PASSES, t=PACK)
+        fk_sb = sb("fk_sb", [P, PASSES, PACK], F32)
+        us_sb = sb("us_sb", [P, PACK], F32)
+        w_raw = [sb(f"w_raw{a}", [P, 2 * R], U8) for a in range(PASSES)]
+        ws_raw = sb("ws_raw", [P, PASSES, R], U8)
+        w_sb = [sb(f"w_sb{a}", [P, 2 * R], U8) for a in range(PASSES)]
+        ws_sb = sb("ws_sb", [P, PASSES, R], U8)
+        wb_sb = sb("wb_sb", [P, N], U32)
+        wbs_sb = sb("wbs_sb", [P, N], U8)
+        old_sb = [sb(f"old{n}", [P, C], F32) for n in range(NT)]
+        page = [sb(f"page{n}", [P, C], F32) for n in range(NT)]
+
+        nc.gpsimd.memset(ws_raw[:].rearrange("p a c -> p (a c)").bitcast(I32), 0)
+        nc.gpsimd.memset(wbs_sb[:].bitcast(I32), 0)
+        for n in range(NT):
+            nc.vector.memset(page[n][:], 0.0)
+
+        def load_plane(i):
+            a, t = divmod(i, PACK)
+            nc.sync.dma_start(out=planes[a][t][:], in_=x_rows[a, t])
+
+        def load_w(a):
+            nc.sync.dma_start(out=w_raw[a][:].bitcast(I32), in_=w_words[a].bitcast(I32))
+
+        load_plane(0)
+        nc.sync.dma_start(second[:], offs2)
+        nc.sync.dma_start(first[:], offs)
+        for q in range(4):
+            nc.scalar.dma_start(
+                out=ws_raw[32 * q : 32 * q + 4].bitcast(I32),
+                in_=w_scales[:, 4 * q : 4 * q + 4, :].rearrange("a r c -> r a c").bitcast(I32),
+            )
+        load_plane(1)
+        load_w(0)
+        load_plane(2)
+        nc.sync.dma_start(out=fk_sb[:], in_=fk.rearrange("(a p t) o -> p a (t o)", a=PASSES, t=PACK))
+        for i in range(3, PASSES * PACK):
+            load_plane(i)
+        load_w(1)
+        nc.sync.dma_start(places[:], offs3)
+        nc.sync.dma_start(out=us_sb[:], in_=us.rearrange("(p t) o -> p (t o)", t=PACK))
+        nc.sync.dma_start(
+            out=wb_sb[:].bitcast(I32), in_=wb_words[0].rearrange("p n t -> p (n t)").bitcast(I32)
+        )
+        for q in range(4):
+            nc.sync.dma_start(
+                out=wbs_sb[32 * q : 32 * q + 4].bitcast(I32),
+                in_=wb_scales[0, 4 * q : 4 * q + 4, :].bitcast(I32),
+            )
+        for n in range(NT):
+            nc.sync.dma_start(out=old_sb[n][:], in_=old[n * P : (n + 1) * P, :])
+
+        nc.vector.tensor_copy(
+            out=ws_sb[:].rearrange("p a (t q) -> p a t q", t=PACK),
+            in_=ws_raw[:].rearrange("p a (q t) -> p a t q", t=PACK),
+        )
+
+        def deal_w(a, copy):
+            copy(
+                out=w_sb[a][:].bitcast(U16).rearrange("p (t q) -> p t q", t=PACK),
+                in_=w_raw[a][:].bitcast(U16).rearrange("p (q t) -> p t q", t=PACK),
+            )
+
+        a_bank = [psum.tile([P, PACK, CH], F32, name=f"a_bank{c}") for c in range(CHUNKS)]
+        p_bank = [psum.tile([P, NT, CH], F32, name=f"p_bank{c}") for c in range(CHUNKS)]
+
+        def quantise(name, woven):
+            width = woven.shape[1]
+            codes = sb(name + "_codes", [P, width], U32)
+            scales = sb(name + "_scales", [P, width], U8)
+            nc.vector.quantize_mx(
+                out=codes[:].bitcast(E4M3), scales=scales[:], in_=woven[:].rearrange("p j t -> p (j t)")
+            )
+            return codes, scales
+
+        def first_product(a, c, codes, scales):
+            for t in range(PACK):
+                nc.tensor.matmul_mx(
+                    out=a_bank[c][:, t, :],
+                    lhsT=w_sb[a][:, 2 * P * t : 2 * P * (t + 1)].bitcast(E2M1),
+                    lhsT_scale=ws_sb[:, a, P * t : P * (t + 1)],
+                    rhs=codes.bitcast(E4M3),
+                    rhs_scale=scales,
+                    start=(a == 0 and t == 0),
+                    stop=(a == PASSES - 1 and t == PACK - 1),
+                )
+
+        gaps = [sb(f"gap{a}", [P, PACK, J], F32) for a in range(PASSES)]
+
+        def gap_plane(a, t, j0, j1, picker):
+            lists = slice(j0 // 16, j1 // 16)
+            taken = sb(f"taken{a}{t}{j0}", [P, j1 - j0], F32)
+            nc.scalar.activation(taken[:], planes[a][t][:].indirect(second[:, lists]), ACT.Copy)
+            minuend = planes[a][t][:].indirect(first[:, lists])
+            if picker is not None:
+                picked = sb(f"picked{a}{t}", [P, j1 - j0], F32)
+                picker(picked[:], minuend)
+                minuend = picked[:]
+            nc.vector.tensor_tensor(gaps[a][:, t, j0:j1], minuend, taken[:], ALU.subtract)
+
+        def weave(a, j0, j1):
+            woven = sb(f"u_woven{a}{j0}", [P, j1 - j0, PACK], BF16)
+            nc.vector.tensor_tensor(
+                woven[:].rearrange("p (c i) t -> p c t i", i=4),
+                gaps[a][:, :, j0:j1].rearrange("p t (c i) -> p c t i", i=4),
+                fk_sb[:, a, :].unsqueeze(1).unsqueeze(3).to_broadcast([P, (j1 - j0) // 4, PACK, 4]),
+                ALU.mult,
+            )
+            return woven
+
+        def scalar_pick(dst, src):
+            nc.scalar.activation(dst, src, ACT.Copy)
+
+        gap_plane(0, 0, 0, J, nc.vector.tensor_copy)
+        deal_w(0, nc.vector.tensor_copy)
+        for t in range(1, PACK):
+            gap_plane(0, t, 0, J, None)
+        codes, scales = quantise("u0", weave(0, 0, J))
+        for c in range(CHUNKS):
+            cols = slice(c * CH, (c + 1) * CH)
+            first_product(0, c, codes[:, cols], scales[:, cols])
+        for t in range(PACK - 1):
+            gap_plane(1, t, 0, J, scalar_pick if PACK + t in BOTH_ON_SCALAR else None)
+        for c in range(CHUNKS):
+            gap_plane(1, PACK - 1, c * CH, (c + 1) * CH, None)
+        deal_w(1, nc.scalar.copy)
+        wovens = [weave(1, 0, CH)]
+        for c in range(CHUNKS):
+            if c + 1 < CHUNKS:
+                wovens.append(weave(1, (c + 1) * CH, (c + 2) * CH))
+            codes, scales = quantise(f"u1{c}", wovens[c])
+            first_product(1, c, codes[:], scales[:])
+
+        last = CHUNKS - 1
+        mags = [sb(f"mag{c}", [P, PACK, CH + 8], F32) for c in range(CHUNKS)]
+        peak = sb("peak", [P, PACK], F32)
+        for c in range(CHUNKS):
+            nc.scalar.activation(mags[c][:, :, 0:CH], a_bank[c][:], ACT.Abs)
+            width = CH + last if c == last else CH
+            dst = peak[:] if c == last else mags[last][:, :, CH + c]
+            nc.vector.tensor_reduce(out=dst, in_=mags[c][:, :, 0:width], axis=AXIS.X, op=ALU.max)
+        inv = sb("inv", [P, PACK], F32)
+        gain = sb("gain", [P, PACK], F32)
+        nc.vector.reciprocal(inv[:], peak[:])
+        nc.vector.tensor_tensor(gain[:], inv[:], us_sb[:], ALU.mult)
+
+        hids = []
+
+        def scale_chunk(c):
+            hid = sb(f"hid{c}", [P, CH, PACK], BF16)
+            nc.vector.tensor_tensor(
+                hid[:],
+                a_bank[c][:].rearrange("p t j -> p j t"),
+                gain[:].unsqueeze(1).to_broadcast([P, CH, PACK]),
+                ALU.mult,
+            )
+            hids.append(hid)
+
+        def second_product(c):
+            codes, scales = quantise(f"hid{c}", hids[c])
+            for n in range(NT):
+                nc.tensor.matmul_mx(
+                    out=p_bank[c][:, n, :],
+                    lhsT=wb_sb[:, n * P : (n + 1) * P].bitcast(E5M2),
+                    lhsT_scale=wbs_sb[:, n * P : (n + 1) * P],
+                    rhs=codes[:].bitcast(E4M3),
+                    rhs_scale=scales[:],
+                    start=True,
+                    stop=True,
+                )
+
+        scale_chunk(0)
+        for c in range(1, CHUNKS):
+            scale_chunk(c)
+            second_product(c - 1)
+        second_product(CHUNKS - 1)
+
+        def where(n, c0, c1):
+            return page[n][:].indirect(places[:, c0 * CH_COLS : c1 * CH_COLS])
+
+        result = sb("result", [P, NT, J], F32)
+        nc.scalar.copy(out=result[:, :, 0:CH], in_=p_bank[0][:])
+        for n in range(NT):
+            nc.scalar.activation(where(n, 0, 1), result[:, n, 0:CH], ACT.Copy)
+        for c in range(1, CHUNKS):
+            nc.vector.tensor_copy(out=result[:, :, c * CH : (c + 1) * CH], in_=p_bank[c][:])
+        for c in range(1, CHUNKS):
+            nc.vector.tensor_copy(where(0, c, c + 1), result[:, 0, c * CH : (c + 1) * CH])
+        nc.scalar.activation(where(1, 1, CHUNKS), result[:, 1, CH:J], ACT.Copy)
+
+        HALF = C // 2
+        for n in range(NT):
+            for h in range(2):
+                cols = slice(h * HALF, (h + 1) * HALF)
+                y = sb(f"y{n}{h}", [P, HALF], F32)
+                nc.vector.scalar_tensor_tensor(
+                    out=y[:], in0=old_sb[n][:, cols], scalar=0.5, in1=page[n][:, cols], op0=ALU.mult, op1=ALU.add
+                )
+                nc.sync.dma_start(out=out[n * P : (n + 1) * P, cols], in_=y[:])

@@ -68,20 +68,21 @@ def tile_list_pickgaps_peakscaled_scattered_kernel(
         def load_w(a):
             nc.sync.dma_start(out=w_raw[a][:].bitcast(I32), in_=w_words[a].bitcast(I32))
 
-        load_plane(0)
         nc.sync.dma_start(second[:], offs2)
         nc.sync.dma_start(first[:], offs)
+        load_plane(0)
         for q in range(4):
             nc.scalar.dma_start(
                 out=ws_raw[32 * q : 32 * q + 4].bitcast(I32),
                 in_=w_scales[:, 4 * q : 4 * q + 4, :].rearrange("a r c -> r a c").bitcast(I32),
             )
         load_plane(1)
-        load_w(0)
         load_plane(2)
         nc.sync.dma_start(out=fk_sb[:], in_=fk.rearrange("(a p t) o -> p a (t o)", a=PASSES, t=PACK))
-        for i in range(3, PASSES * PACK):
+        for i in range(3, PASSES * PACK - 1):
             load_plane(i)
+        load_w(0)
+        load_plane(PASSES * PACK - 1)
         load_w(1)
         nc.sync.dma_start(places[:], offs3)
         nc.sync.dma_start(out=us_sb[:], in_=us.rearrange("(p t) o -> p (t o)", t=PACK))
@@ -157,16 +158,15 @@ def tile_list_pickgaps_peakscaled_scattered_kernel(
         def scalar_pick(dst, src):
             nc.scalar.activation(dst, src, ACT.Copy)
 
-        gap_plane(0, 0, 0, J, nc.vector.tensor_copy)
-        deal_w(0, nc.vector.tensor_copy)
-        for t in range(1, PACK):
+        for t in range(PACK):
             gap_plane(0, t, 0, J, None)
         codes, scales = quantise("u0", weave(0, 0, J))
+        for t in range(PACK - 1):
+            gap_plane(1, t, 0, J, scalar_pick if PACK + t in BOTH_ON_SCALAR else None)
+        deal_w(0, nc.scalar.copy)
         for c in range(CHUNKS):
             cols = slice(c * CH, (c + 1) * CH)
             first_product(0, c, codes[:, cols], scales[:, cols])
-        for t in range(PACK - 1):
-            gap_plane(1, t, 0, J, scalar_pick if PACK + t in BOTH_ON_SCALAR else None)
         for c in range(CHUNKS):
             gap_plane(1, PACK - 1, c * CH, (c + 1) * CH, None)
         deal_w(1, nc.scalar.copy)
@@ -226,19 +226,17 @@ def tile_list_pickgaps_peakscaled_scattered_kernel(
 
         result = sb("result", [P, NT, J], F32)
         nc.scalar.copy(out=result[:, :, 0:CH], in_=p_bank[0][:])
-        for n in range(NT):
-            nc.scalar.activation(where(n, 0, 1), result[:, n, 0:CH], ACT.Copy)
+        nc.scalar.activation(where(0, 0, 1), result[:, 0, 0:CH], ACT.Copy)
         for c in range(1, CHUNKS):
             nc.vector.tensor_copy(out=result[:, :, c * CH : (c + 1) * CH], in_=p_bank[c][:])
-        for c in range(1, CHUNKS):
-            nc.vector.tensor_copy(where(0, c, c + 1), result[:, 0, c * CH : (c + 1) * CH])
-        nc.scalar.activation(where(1, 1, CHUNKS), result[:, 1, CH:J], ACT.Copy)
+        nc.vector.tensor_copy(where(0, 1, CHUNKS), result[:, 0, CH:J])
+        nc.scalar.activation(where(1, 0, CHUNKS), result[:, 1, :], ACT.Copy)
 
-        HALF = C // 2
+        pieces = [(0, C // 2, C), (0, C // 2, 3 * C // 4, C)]
         for n in range(NT):
-            for h in range(2):
-                cols = slice(h * HALF, (h + 1) * HALF)
-                y = sb(f"y{n}{h}", [P, HALF], F32)
+            for c0, c1 in zip(pieces[n], pieces[n][1:]):
+                cols = slice(c0, c1)
+                y = sb(f"y{n}{c0}", [P, c1 - c0], F32)
                 nc.vector.scalar_tensor_tensor(
                     out=y[:], in0=old_sb[n][:, cols], scalar=0.5, in1=page[n][:, cols], op0=ALU.mult, op1=ALU.add
                 )

@@ -26,7 +26,7 @@ CHUNKS = J // CH
 NT = N // P
 LIST_COLS = J // 16
 CH_COLS = CH // 16
-BOTH_ON_SCALAR = (4,)
+BOTH_ON_SCALAR = ()
 
 
 def tile_list_pickgaps_peakscaled_scattered_kernel(
@@ -76,13 +76,12 @@ def tile_list_pickgaps_peakscaled_scattered_kernel(
                 out=ws_raw[32 * q : 32 * q + 4].bitcast(I32),
                 in_=w_scales[:, 4 * q : 4 * q + 4, :].rearrange("a r c -> r a c").bitcast(I32),
             )
+        load_w(0)
         load_plane(1)
         load_plane(2)
         nc.sync.dma_start(out=fk_sb[:], in_=fk.rearrange("(a p t) o -> p a (t o)", a=PASSES, t=PACK))
-        for i in range(3, PASSES * PACK - 1):
+        for i in range(3, PASSES * PACK):
             load_plane(i)
-        load_w(0)
-        load_plane(PASSES * PACK - 1)
         load_w(1)
         nc.sync.dma_start(places[:], offs3)
         nc.sync.dma_start(out=us_sb[:], in_=us.rearrange("(p t) o -> p (t o)", t=PACK))
@@ -158,12 +157,12 @@ def tile_list_pickgaps_peakscaled_scattered_kernel(
         def scalar_pick(dst, src):
             nc.scalar.activation(dst, src, ACT.Copy)
 
+        deal_w(0, nc.vector.tensor_copy)
         for t in range(PACK):
             gap_plane(0, t, 0, J, None)
         codes, scales = quantise("u0", weave(0, 0, J))
         for t in range(PACK - 1):
             gap_plane(1, t, 0, J, scalar_pick if PACK + t in BOTH_ON_SCALAR else None)
-        deal_w(0, nc.scalar.copy)
         for c in range(CHUNKS):
             cols = slice(c * CH, (c + 1) * CH)
             first_product(0, c, codes[:, cols], scales[:, cols])

@@ -26,7 +26,7 @@ CHUNKS = J // CH
 NT = N // P
 LIST_COLS = J // 16
 CH_COLS = CH // 16
-BOTH_ON_SCALAR = ()
+BOTH_ON_SCALAR = (4,)
 
 
 def tile_list_pickgaps_peakscaled_scattered_kernel(
@@ -224,14 +224,15 @@ def tile_list_pickgaps_peakscaled_scattered_kernel(
             return page[n][:].indirect(places[:, c0 * CH_COLS : c1 * CH_COLS])
 
         result = sb("result", [P, NT, J], F32)
-        nc.scalar.copy(out=result[:, :, 0:CH], in_=p_bank[0][:])
+        nc.scalar.copy(out=result[:, 0, 0:CH], in_=p_bank[0][:, 0, :])
+        nc.scalar.copy(out=result[:, 1, 0:CH], in_=p_bank[0][:, 1, :])
         nc.scalar.activation(where(0, 0, 1), result[:, 0, 0:CH], ACT.Copy)
         for c in range(1, CHUNKS):
             nc.vector.tensor_copy(out=result[:, :, c * CH : (c + 1) * CH], in_=p_bank[c][:])
         nc.vector.tensor_copy(where(0, 1, CHUNKS), result[:, 0, CH:J])
         nc.scalar.activation(where(1, 0, CHUNKS), result[:, 1, :], ACT.Copy)
 
-        pieces = [(0, C // 2, C), (0, C // 2, 3 * C // 4, C)]
+        pieces = [(0, C // 2, C), (0, C // 2, C)]
         for n in range(NT):
             for c0, c1 in zip(pieces[n], pieces[n][1:]):
                 cols = slice(c0, c1)

from contextlib import ExitStack

import concourse.mybir as mybir

K, T, J, R, N, C = 1024, 1024, 384, 512, 256, 1024
FLOPS = 2 * K * R * J + 2 * R * N * J

F32 = mybir.dt.float32
BF16 = mybir.dt.bfloat16
I32 = mybir.dt.int32
U32 = mybir.dt.uint32
U16 = mybir.dt.uint16
U8 = mybir.dt.uint8
E4M3 = mybir.dt.float8_e4m3fn_x4
E5M2 = mybir.dt.float8_e5m2_x4
E2M1 = mybir.dt.float4_e2m1fn_x4
ALU = mybir.AluOpType
ACT = mybir.ActivationFunctionType
AXIS = mybir.AxisListType

P = 128
PACK = 4
PASSES = K // (P * PACK)
CH = 128
CHUNKS = J // CH
NT = N // P
LIST_COLS = J // 16
CH_COLS = CH // 16
BOTH_ON_SCALAR = (4,)


def tile_list_pickgaps_peakscaled_scattered_kernel(
    tc, xf, fk, w_words, w_scales, us, wb_words, wb_scales, old, offs, offs2, offs3, out
):
    nc = tc.nc
    with ExitStack() as ctx:
        keep = ctx.enter_context(tc.tile_pool(name="keep", bufs=1))
        psum = ctx.enter_context(tc.psum_pool(name="psum", bufs=1))

        def sb(name, shape, dtype):
            return keep.tile(shape, dtype, name=name, align_bytes=64)

        first = keep.tile([P, LIST_COLS], U16, name="first")
        second = keep.tile([P, LIST_COLS], U16, name="second")
        places = keep.tile([P, LIST_COLS], U16, name="places")
        planes = [[sb(f"x{a}{t}", [P, T], F32) for t in range(PACK)] for a in range(PASSES)]
        x_rows = xf.rearrange("(a p t) c -> a t p c", a=PASSES, t=PACK)
        fk_sb = sb("fk_sb", [P, PASSES, PACK], F32)
        us_sb = sb("us_sb", [P, PACK], F32)
        w_raw = [sb(f"w_raw{a}", [P, 2 * R], U8) for a in range(PASSES)]
        ws_raw = sb("ws_raw", [P, PASSES, R], U8)
        w_sb = [sb(f"w_sb{a}", [P, 2 * R], U8) for a in range(PASSES)]
        ws_sb = sb("ws_sb", [P, PASSES, R], U8)
        wb_sb = sb("wb_sb", [P, N], U32)
        wbs_sb = sb("wbs_sb", [P, N], U8)
        old_sb = [sb(f"old{n}", [P, C], F32) for n in range(NT)]
        page = [sb(f"page{n}", [P, C], F32) for n in range(NT)]

        nc.gpsimd.memset(ws_raw[:].rearrange("p a c -> p (a c)").bitcast(I32), 0)
        nc.gpsimd.memset(wbs_sb[:].bitcast(I32), 0)
        for n in range(NT):
            nc.vector.memset(page[n][:], 0.0)

        def load_plane(i):
            a, t = divmod(i, PACK)
            nc.sync.dma_start(out=planes[a][t][:], in_=x_rows[a, t])

        def load_w(a):
            nc.sync.dma_start(out=w_raw[a][:].bitcast(I32), in_=w_words[a].bitcast(I32))

        nc.sync.dma_start(second[:], offs2)
        nc.sync.dma_start(first[:], offs)
        load_plane(0)
        for q in range(4):
            nc.scalar.dma_start(
                out=ws_raw[32 * q : 32 * q + 4].bitcast(I32),
                in_=w_scales[:, 4 * q : 4 * q + 4, :].rearrange("a r c -> r a c").bitcast(I32),
            )
        load_w(0)
        load_plane(1)
        load_plane(2)
        nc.sync.dma_start(out=fk_sb[:], in_=fk.rearrange("(a p t) o -> p a (t o)", a=PASSES, t=PACK))
        for i in range(3, PASSES * PACK):
            load_plane(i)
        load_w(1)
        nc.sync.dma_start(places[:], offs3)
        nc.sync.dma_start(out=us_sb[:], in_=us.rearrange("(p t) o -> p (t o)", t=PACK))
        nc.sync.dma_start(
            out=wb_sb[:].bitcast(I32), in_=wb_words[0].rearrange("p n t -> p (n t)").bitcast(I32)
        )
        for q in range(4):
            nc.sync.dma_start(
                out=wbs_sb[32 * q : 32 * q + 4].bitcast(I32),
                in_=wb_scales[0, 4 * q : 4 * q + 4, :].bitcast(I32),
            )
        for n in range(NT):
            nc.sync.dma_start(out=old_sb[n][:], in_=old[n * P : (n + 1) * P, :])

        nc.vector.tensor_copy(
            out=ws_sb[:].rearrange("p a (t q) -> p a t q", t=PACK),
            in_=ws_raw[:].rearrange("p a (q t) -> p a t q", t=PACK),
        )

        def deal_w(a, copy):
            copy(
                out=w_sb[a][:].bitcast(U16).rearrange("p (t q) -> p t q", t=PACK),
                in_=w_raw[a][:].bitcast(U16).rearrange("p (q t) -> p t q", t=PACK),
            )

        a_bank = [psum.tile([P, PACK, CH], F32, name=f"a_bank{c}") for c in range(CHUNKS)]
        p_bank = [psum.tile([P, NT, CH], F32, name=f"p_bank{c}") for c in range(CHUNKS)]

        def quantise(name, woven):
            width = woven.shape[1]
            codes = sb(name + "_codes", [P, width], U32)
            scales = sb(name + "_scales", [P, width], U8)
            nc.vector.quantize_mx(
                out=codes[:].bitcast(E4M3), scales=scales[:], in_=woven[:].rearrange("p j t -> p (j t)")
            )
            return codes, scales

        def first_product(a, c, codes, scales):
            for t in range(PACK):
                nc.tensor.matmul_mx(
                    out=a_bank[c][:, t, :],
                    lhsT=w_sb[a][:, 2 * P * t : 2 * P * (t + 1)].bitcast(E2M1),
                    lhsT_scale=ws_sb[:, a, P * t : P * (t + 1)],
                    rhs=codes.bitcast(E4M3),
                    rhs_scale=scales,
                    start=(a == 0 and t == 0),
                    stop=(a == PASSES - 1 and t == PACK - 1),
                )

        gaps = [sb(f"gap{a}", [P, PACK, J], F32) for a in range(PASSES)]

        def gap_plane(a, t, j0, j1, picker):
            lists = slice(j0 // 16, j1 // 16)
            taken = sb(f"taken{a}{t}{j0}", [P, j1 - j0], F32)
            nc.scalar.activation(taken[:], planes[a][t][:].indirect(second[:, lists]), ACT.Copy)
            minuend = planes[a][t][:].indirect(first[:, lists])
            if picker is not None:
                picked = sb(f"picked{a}{t}", [P, j1 - j0], F32)
                picker(picked[:], minuend)
                minuend = picked[:]
            nc.vector.tensor_tensor(gaps[a][:, t, j0:j1], minuend, taken[:], ALU.subtract)

        def weave(a, j0, j1):
            woven = sb(f"u_woven{a}{j0}", [P, j1 - j0, PACK], BF16)
            nc.vector.tensor_tensor(
                woven[:].rearrange("p (c i) t -> p c t i", i=4),
                gaps[a][:, :, j0:j1].rearrange("p t (c i) -> p c t i", i=4),
                fk_sb[:, a, :].unsqueeze(1).unsqueeze(3).to_broadcast([P, (j1 - j0) // 4, PACK, 4]),
                ALU.mult,
            )
            return woven

        def scalar_pick(dst, src):
            nc.scalar.activation(dst, src, ACT.Copy)

        deal_w(0, nc.vector.tensor_copy)
        for t in range(PACK):
            gap_plane(0, t, 0, J, None)
        codes, scales = quantise("u0", weave(0, 0, J))
        for t in range(PACK - 1):
            gap_plane(1, t, 0, J, scalar_pick if PACK + t in BOTH_ON_SCALAR else None)
        for c in range(CHUNKS):
            cols = slice(c * CH, (c + 1) * CH)
            first_product(0, c, codes[:, cols], scales[:, cols])
        for c in range(CHUNKS):
            gap_plane(1, PACK - 1, c * CH, (c + 1) * CH, None)
        deal_w(1, nc.scalar.copy)
        wovens = [weave(1, 0, CH)]
        for c in range(CHUNKS):
            if c + 1 < CHUNKS:
                wovens.append(weave(1, (c + 1) * CH, (c + 2) * CH))
            codes, scales = quantise(f"u1{c}", wovens[c])
            first_product(1, c, codes[:], scales[:])

        last = CHUNKS - 1
        mags = [sb(f"mag{c}", [P, PACK, CH + 8], F32) for c in range(CHUNKS)]
        peak = sb("peak", [P, PACK], F32)
        for c in range(CHUNKS):
            nc.scalar.activation(mags[c][:, :, 0:CH], a_bank[c][:], ACT.Abs)
            width = CH + last if c == last else CH
            dst = peak[:] if c == last else mags[last][:, :, CH + c]
            nc.vector.tensor_reduce(out=dst, in_=mags[c][:, :, 0:width], axis=AXIS.X, op=ALU.max)
        inv = sb("inv", [P, PACK], F32)
        gain = sb("gain", [P, PACK], F32)
        nc.vector.reciprocal(inv[:], peak[:])
        nc.vector.tensor_tensor(gain[:], inv[:], us_sb[:], ALU.mult)

        hids = []

        def scale_chunk(c):
            hid = sb(f"hid{c}", [P, CH, PACK], BF16)
            nc.vector.tensor_tensor(
                hid[:],
                a_bank[c][:].rearrange("p t j -> p j t"),
                gain[:].unsqueeze(1).to_broadcast([P, CH, PACK]),
                ALU.mult,
            )
            hids.append(hid)

        def second_product(c):
            codes, scales = quantise(f"hid{c}", hids[c])
            for n in range(NT):
                nc.tensor.matmul_mx(
                    out=p_bank[c][:, n, :],
                    lhsT=wb_sb[:, n * P : (n + 1) * P].bitcast(E5M2),
                    lhsT_scale=wbs_sb[:, n * P : (n + 1) * P],
                    rhs=codes[:].bitcast(E4M3),
                    rhs_scale=scales[:],
                    start=True,
                    stop=True,
                )

        scale_chunk(0)
        for c in range(1, CHUNKS):
            scale_chunk(c)
            second_product(c - 1)
        second_product(CHUNKS - 1)

        def where(n, c0, c1):
            return page[n][:].indirect(places[:, c0 * CH_COLS : c1 * CH_COLS])

        result = sb("result", [P, NT, J], F32)
        nc.scalar.copy(out=result[:, 0, 0:CH], in_=p_bank[0][:, 0, :])
        nc.scalar.copy(out=result[:, 1, 0:CH], in_=p_bank[0][:, 1, :])
        nc.scalar.activation(where(0, 0, 1), result[:, 0, 0:CH], ACT.Copy)
        for c in range(1, CHUNKS):
            nc.vector.tensor_copy(out=result[:, :, c * CH : (c + 1) * CH], in_=p_bank[c][:])
        nc.vector.tensor_copy(where(0, 1, CHUNKS), result[:, 0, CH:J])
        nc.scalar.activation(where(1, 0, CHUNKS), result[:, 1, :], ACT.Copy)

        pieces = [(0, C // 2, C), (0, C // 2, C)]
        for n in range(NT):
            for c0, c1 in zip(pieces[n], pieces[n][1:]):
                cols = slice(c0, c1)
                y = sb(f"y{n}{c0}", [P, c1 - c0], F32)
                nc.vector.scalar_tensor_tensor(
                    out=y[:], in0=old_sb[n][:, cols], scalar=0.5, in1=page[n][:, cols], op0=ALU.mult, op1=ALU.add
                )
                nc.sync.dma_start(out=out[n * P : (n + 1) * P, cols], in_=y[:])
